import numpy as np
import ml_dtypes


def mxq(x, axis, fmt="e4m3"):
    dtype, down = {"e4m3": (ml_dtypes.float8_e4m3fn, 7), "e5m2": (ml_dtypes.float8_e5m2, 14)}[fmt]
    v = np.moveaxis(np.asarray(x, np.float32).astype(ml_dtypes.bfloat16).astype(np.float64), axis, -1)
    blocks = v.reshape(v.shape[:-1] + (-1, 32))
    amax = np.abs(blocks).max(-1, keepdims=True)
    byte = np.maximum(np.where(amax > 0, np.frexp(amax)[1] - 1 + 127, 0) - down, 1)
    scale = np.exp2(byte - 127.0)
    codes = (blocks / scale).astype(np.float32).astype(dtype).astype(np.float64)
    return np.moveaxis((codes * scale).reshape(v.shape), -1, axis)


WIDE = False


def mx_kscale(k):
    if not WIDE:
        return np.ones(k)
    levels = np.array([10, -10, 5, -5, 0])
    if k % 512:
        return np.exp2(np.random.permutation(np.resize(levels, k // 32))).repeat(32)
    a = np.empty((k // 512, 16))
    for p in range(k // 512):
        a[p, :8] = np.random.permutation(np.resize(levels, 8))
        for g in range(8):
            far = levels[np.abs(levels - a[p, g]) >= 10]
            a[p, g + 8] = far[np.random.randint(len(far))]
    return np.exp2(a.ravel()).repeat(32)


def f64(x):
    return np.asarray(x).astype(np.float64)


def striped(idx):
    return np.tile(idx.reshape(-1, 16).T, (8, 1)).astype(np.uint16)


def unstriped(offs):
    return offs[:16].T.reshape(-1).astype(np.int64)


def striped8(idx):
    return np.concatenate([x.reshape(-1, 16).T for x in idx]).astype(np.uint16)


def runs(offs, k):
    lists = np.stack([offs[16 * r : 16 * r + 16].T.reshape(-1) for r in range(8)]).astype(np.int64)
    return lists[np.arange(k) % 512 // 64]


def pack_weight(w):
    k, n = w.shape
    w = f64(np.asarray(w, np.float32).astype(ml_dtypes.bfloat16)).reshape(k // 32, 32, n)
    amax = np.abs(w).max(1)
    byte = np.clip(np.where(amax > 0, np.frexp(amax)[1] - 1 + 127 - 7, 1), 1, 254)
    scaled = (w * np.exp2(127.0 - byte)[:, None, :]).reshape(k, n).astype(np.float32)
    words = np.ascontiguousarray(scaled.reshape(k // 512, 128, 4, n).transpose(0, 1, 3, 2)).astype(ml_dtypes.float8_e4m3fn).view(np.uint8)
    return words, np.ascontiguousarray(byte.astype(np.uint8).reshape(k // 512, 16, n))


def unpack_weight(words, scales):
    g, p, n, _ = words.shape
    vals = np.ascontiguousarray(words).view(ml_dtypes.float8_e4m3fn).astype(np.float64) * np.repeat(np.exp2(scales.astype(np.float64) - 127.0), 8, axis=1)[..., None]
    return vals.transpose(0, 1, 3, 2).reshape(g * 512, n)


K, T, S, N, G, H, W = 512, 1024, 256, 512, 2048, 512, 128


def setup_inputs():
    n = np.random.standard_normal
    s = mx_kscale(K)[:, None]
    u = mx_kscale(K)
    packed_xT = pack_weight(n((K, T)) * s)
    packed_dT = pack_weight(n((K, G)) / s)
    perm = np.random.permutation(S)
    return {
        "x_words": packed_xT[0],
        "x_scales": packed_xT[1],
        "d_words": packed_dT[0],
        "d_scales": packed_dT[1],
        "gn": (np.random.uniform(0.5, 1.5, (H, 1)) * u[:, None]).astype(np.float32),
        "w1": (n((H, N)) / np.sqrt(2 * H) / u[:, None]).astype(np.float32),
        "w2": (n((K, N)) / np.sqrt(2 * K) / s).astype(np.float32),
        "offs": striped8(np.random.randint(0, T, (8, S))),
        "ci": striped(np.random.permutation(G)[:H]),
        "n1": striped(np.random.permutation(S)),
        "n2": striped(np.random.permutation(S)),
        "n3": striped(np.random.permutation(S)),
        "hz": striped8(np.random.randint(0, T, (8, S))),
        "n4": striped(perm[:W]),
        "n5": striped(perm[W:]),
    }


def reference(x_words, x_scales, d_words, d_scales, gn, w1, w2, offs, ci, n1, n2, n3, hz, n4, n5):
    d_ci = unpack_weight(d_words, d_scales)[:, unstriped(ci)]
    xq = unpack_weight(x_words, x_scales)[np.arange(K)[:, None], runs(offs, K)]
    s = 0.0625 * (d_ci.T @ xq)
    ds = np.zeros((H, S))
    ds[:, unstriped(n1)] = s
    st = np.minimum(ds, s[:, unstriped(n2)])
    z = f64(gn) * (st - st[:, unstriped(n3)])
    x_hz = unpack_weight(x_words, x_scales)[np.arange(K)[:, None], runs(hz, K)]
    h2 = mxq(f64(w1), 0, "e4m3").T @ mxq(z, 0, "e4m3") + mxq(f64(w2), 0, "e4m3").T @ x_hz
    pb = h2[:, unstriped(n5)]
    pa = h2[:, unstriped(n4)]
    rb = pb - (0.5 * pa)
    ra = np.sqrt((pa) ** 2 + (pb) ** 2 + 0.25)
    ua = np.zeros((N, S))
    ua[:, unstriped(n4)] = ra
    out = ua.copy()
    out[:, unstriped(n5)] = rb
    return out

@@ -1,0 +1,196 @@
+from contextlib import ExitStack
+
+import concourse.mybir as mybir
+
+F32 = mybir.dt.float32
+BF16 = mybir.dt.bfloat16
+I32 = mybir.dt.int32
+U32 = mybir.dt.uint32
+U16 = mybir.dt.uint16
+U8 = mybir.dt.uint8
+FP8X4 = mybir.dt.float8_e4m3fn_x4
+ALU = mybir.AluOpType
+ACT = mybir.ActivationFunctionType
+
+P = 128
+PACK = 4
+K, T, S, N, G, H, W = 512, 1024, 256, 512, 2048, 512, 128
+HALF = S // 2
+SPARE = 16
+FLOPS = 2 * S * (K * H + H * N + K * N)
+
+
+def tile_picked_xhznhsndminpolar_none_p_kernel(
+    tc, x_words, x_scales, d_words, d_scales, gn, w1, w2, offs, ci, n1, n2, n3, hz, n4, n5, out
+):
+    nc = tc.nc
+    with ExitStack() as ctx:
+        lists = ctx.enter_context(tc.tile_pool(name="lists", bufs=1))
+        sb = ctx.enter_context(tc.tile_pool(name="sb", bufs=1))
+        psum = ctx.enter_context(tc.psum_pool(name="psum", bufs=1))
+
+        def load_list(name, src):
+            tile = lists.tile(list(src.shape), U16, name=name)
+            nc.sync.dma_start(tile[:], src)
+            return tile
+
+        def load_words(name, src, width):
+            tile = sb.tile([P, width], U32, name=name, tag=name, align_bytes=64)
+            nc.sync.dma_start(tile[:].bitcast(I32), src[0].rearrange("p n t -> p (n t)").bitcast(I32))
+            return tile
+
+        def load_scales(name, src, width, clear):
+            tile = sb.tile([P, width], U8, name=name, tag=name, align_bytes=64)
+            clear.memset(tile[:].bitcast(I32), 0)
+            nc.scalar.dma_start(tile[0:P:8, :].bitcast(I32), src[0].bitcast(I32))
+            return tile
+
+        def place_scale_rows(name, picked, width, queue):
+            placed = sb.tile([P, width], U8, name=name, align_bytes=64)
+            nc.gpsimd.memset(placed[:].bitcast(I32), 0)
+            for r in range(4):
+                queue.dma_start(placed[r:P:32, :].bitcast(I32), picked[8 * r:P:32, :].bitcast(I32))
+            return placed
+
+        xs_table = load_scales("xs_table", x_scales, T, nc.gpsimd)
+        ds_table = load_scales("ds_table", d_scales, G, nc.vector)
+        offs_t = load_list("offs_t", offs)
+        ci_t = load_list("ci_t", ci)
+        d_table = load_words("d_table", d_words, G)
+        n1_t = load_list("n1_t", n1)
+        n2_t = load_list("n2_t", n2)
+        hz_t = load_list("hz_t", hz)
+        x_table = load_words("x_table", x_words, T)
+        n3_t = load_list("n3_t", n3)
+        n4_t = load_list("n4_t", n4)
+        n5_t = load_list("n5_t", n5)
+        gain = sb.tile([P, PACK], F32, name="gain")
+        nc.gpsimd.dma_start(gain[:], gn.rearrange("(p t) o -> p (t o)", t=PACK))
+
+        bytes1 = sb.tile([P, H + S], U8, name="bytes1", align_bytes=64)
+        nc.vector.tensor_copy(bytes1[:, H:], xs_table[:].indirect(offs_t[:]))
+        nc.vector.tensor_copy(bytes1[:, :H].rearrange("p (t m) -> p m t", t=PACK), ds_table[:].indirect(ci_t[:]))
+        scale1 = place_scale_rows("scale1", bytes1, H + S, nc.scalar)
+        d_codes = sb.tile([P, H], U32, name="d_codes", align_bytes=64)
+        nc.vector.tensor_copy(d_codes[:].rearrange("p (t m) -> p m t", t=PACK), d_table[:].indirect(ci_t[:]))
+        x_codes = sb.tile([P, S], U32, name="x_codes", align_bytes=64)
+        nc.vector.tensor_copy(x_codes[:], x_table[:].indirect(offs_t[:]))
+
+        w2_raw = sb.tile([P, PACK, N], F32, name="w2_raw", tag="ds_table", align_bytes=64)
+        nc.sync.dma_start(w2_raw[:], w2.rearrange("(p j) n -> p j n", j=PACK))
+        w1_raw = sb.tile([P, PACK, N], F32, name="w1_raw", tag="d_table", align_bytes=64)
+        nc.sync.dma_start(w1_raw[:], w1.rearrange("(p j) n -> p j n", j=PACK))
+
+        s_t = []
+        for t in range(PACK):
+            bank = psum.tile([P, S], F32, name="s_bank%d" % t, tag="bank%d" % t)
+            cols = slice(P * t, P * (t + 1))
+            nc.tensor.matmul_mx(
+                out=bank[:], lhsT=d_codes[:, cols].bitcast(FP8X4), lhsT_scale=scale1[:, cols],
+                rhs=x_codes[:].bitcast(FP8X4), rhs_scale=scale1[:, H:], start=True, stop=True,
+            )
+            s = sb.tile([P, S + SPARE], F32, name="s%d" % t)
+            nc.gpsimd.memset(s[:, S:], 0.0)
+            nc.vector.tensor_scalar(s[:, :S], bank[:], 0.0625, None, ALU.mult)
+            s_t.append(s)
+
+        bytes2 = sb.tile([P, S], U8, name="bytes2", align_bytes=64)
+        nc.vector.tensor_copy(bytes2[:], xs_table[:].indirect(hz_t[:]))
+        scale2 = place_scale_rows("scale2", bytes2, S, nc.sync)
+        hz_codes = sb.tile([P, S], U32, name="hz_codes", align_bytes=64)
+        nc.vector.tensor_copy(hz_codes[:], x_table[:].indirect(hz_t[:]))
+
+        def quantise_weight(name, raw):
+            grouped = sb.tile([P, N * PACK], BF16, name=name + "_grouped", tag="stage", align_bytes=64)
+            nc.vector.tensor_copy(
+                grouped[:].rearrange("p (c i t) -> p c t i", i=4, t=PACK),
+                raw[:].rearrange("p t (c i) -> p c t i", i=4),
+            )
+            codes = sb.tile([P, N], U32, name=name + "_codes", align_bytes=64)
+            scales = sb.tile([P, N], U8, name=name + "_scales", align_bytes=64)
+            nc.vector.quantize_mx(out=codes[:].bitcast(FP8X4), scales=scales[:], in_=grouped[:])
+            return codes, scales
+
+        w2_codes, w2_scales = quantise_weight("w2", w2_raw)
+        w1_codes, w1_scales = quantise_weight("w1", w1_raw)
+
+        st = sb.tile([P, PACK * S], F32, name="st", tag="stage", align_bytes=64)
+        stg = sb.tile([P, PACK * S], F32, name="stg")
+        for t in range(PACK):
+            cols = slice(S * t, S * (t + 1))
+            ds = sb.tile([P, 2 * S], F32, name="ds%d" % t)
+            nc.scalar.activation(ds[:].indirect(n1_t[:]), s_t[t][:, :S], ACT.Copy)
+            s2 = sb.tile([P, S], F32, name="s2_%d" % t)
+            nc.scalar.activation(s2[:], s_t[t][:].indirect(n2_t[:]), ACT.Copy)
+            nc.vector.tensor_tensor(st[:, cols], ds[:, :S], s2[:], ALU.min)
+            nc.vector.tensor_scalar(stg[:, cols], st[:, cols], gain[:, t:t + 1], None, ALU.mult)
+
+        first_bank = psum.tile([P, PACK, HALF], F32, name="first_bank")
+        acc = [[first_bank[:, m, :] for m in range(PACK)], []]
+        for m in range(PACK):
+            second_bank = psum.tile([P, HALF], F32, name="second_bank%d" % m, tag="bank%d" % m)
+            acc[1].append(second_bank[:])
+        for h in range(2):
+            for m in range(PACK):
+                rows = slice(P * m, P * (m + 1))
+                cols = slice(HALF * h, HALF * (h + 1))
+                nc.tensor.matmul_mx(
+                    out=acc[h][m], lhsT=w2_codes[:, rows].bitcast(FP8X4), lhsT_scale=w2_scales[:, rows],
+                    rhs=hz_codes[:, cols].bitcast(FP8X4), rhs_scale=scale2[:, cols],
+                    start=(h == 1 or m == 0), stop=False,
+                )
+
+        h2 = sb.tile([P, PACK * S], F32, name="h2")
+        h2_view = h2[:].rearrange("p (m c) -> p m c", m=PACK)
+        for h in range(2):
+            st3 = sb.tile([P, PACK * HALF], F32, name="st3_%d" % h)
+            for t in range(PACK):
+                nc.scalar.activation(
+                    st3[:, HALF * t:HALF * (t + 1)],
+                    stg[:, S * t:S * (t + 1)].indirect(n3_t[:, 8 * h:8 * (h + 1)]), ACT.Copy,
+                )
+            z = sb.tile([P, HALF * PACK], BF16, name="z%d" % h, align_bytes=64)
+            nc.vector.tensor_tensor(
+                z[:].rearrange("p (c i t) -> p c t i", i=4, t=PACK),
+                stg[:].rearrange("p (t h c i) -> p h c t i", t=PACK, h=2, i=4)[:, h],
+                st3[:].rearrange("p (t c i) -> p c t i", t=PACK, i=4),
+                ALU.subtract,
+            )
+            z_codes = sb.tile([P, HALF], U32, name="z_codes%d" % h, align_bytes=64)
+            z_scales = sb.tile([P, HALF], U8, name="z_scales%d" % h, align_bytes=64)
+            nc.vector.quantize_mx(out=z_codes[:].bitcast(FP8X4), scales=z_scales[:], in_=z[:])
+            for m in range(PACK):
+                rows = slice(P * m, P * (m + 1))
+                nc.tensor.matmul_mx(
+                    out=acc[h][m], lhsT=w1_codes[:, rows].bitcast(FP8X4), lhsT_scale=w1_scales[:, rows],
+                    rhs=z_codes[:].bitcast(FP8X4), rhs_scale=z_scales[:],
+                    start=False, stop=(h == 1 or m == PACK - 1),
+                )
+        nc.scalar.copy(h2_view[:, :, :HALF], first_bank[:])
+        nc.scalar.copy(h2_view[:, 0, HALF:], acc[1][0])
+        for m in range(1, PACK):
+            nc.vector.tensor_copy(h2_view[:, m, HALF:], acc[1][m])
+
+        pairs = sb.tile([P, PACK, 2, W], F32, name="pairs")
+        squares = sb.tile([P, PACK, 2, W], F32, name="squares")
+        radicand = sb.tile([P, PACK * W], F32, name="radicand")
+        rb = sb.tile([P, PACK, W], F32, name="rb")
+        ra = sb.tile([P, PACK * W], F32, name="ra")
+        for m in range(PACK):
+            window = h2[:, S * m:S * (m + 1)]
+            nc.scalar.activation(pairs[:, m, 0, :], window.indirect(n4_t[:]), ACT.Copy)
+            nc.scalar.activation(pairs[:, m, 1, :], window.indirect(n5_t[:]), ACT.Copy)
+            nc.vector.scalar_tensor_tensor(rb[:, m, :], pairs[:, m, 0, :], -0.5, pairs[:, m, 1, :], ALU.mult, ALU.add)
+            nc.vector.tensor_tensor(squares[:, m], pairs[:, m], pairs[:, m], ALU.mult)
+            nc.vector.scalar_tensor_tensor(
+                radicand[:, W * m:W * (m + 1)], squares[:, m, 0, :], 0.25, squares[:, m, 1, :], ALU.add, ALU.add
+            )
+        results = [sb.tile([P, S], F32, name="result%d" % m) for m in range(PACK)]
+        for m in range(2):
+            nc.scalar.activation(results[m][:].indirect(n5_t[:]), rb[:, m, :], ACT.Copy)
+        nc.scalar.activation(ra[:], radicand[:], ACT.Sqrt)
+        for m in range(PACK):
+            nc.scalar.activation(results[m][:].indirect(n4_t[:]), ra[:, W * m:W * (m + 1)], ACT.Copy)
+            nc.sync.dma_start(out[P * m:P * (m + 1), :], results[m][:])
+            if m + 2 < PACK:
+                nc.scalar.activation(results[m + 2][:].indirect(n5_t[:]), rb[:, m + 2, :], ACT.Copy)

@@ -54,6 +54,10 @@ def tile_picked_xhznhsndminpolar_none_p_kernel(
 
         xs_table = load_scales("xs_table", x_scales, T, nc.gpsimd)
         ds_table = load_scales("ds_table", d_scales, G, nc.vector)
+        one = sb.tile([P, 1], F32, name="one")
+        nc.vector.memset(one[:], 1.0)
+        root_of_one = sb.tile([P, 1], F32, name="root_of_one")
+        nc.scalar.activation(root_of_one[:], one[:], ACT.Sqrt)
         offs_t = load_list("offs_t", offs)
         ci_t = load_list("ci_t", ci)
         d_table = load_words("d_table", d_words, G)

@@ -39,68 +39,74 @@ def tile_picked_xhznhsndminpolar_none_p_kernel(
             nc.sync.dma_start(tile[:].bitcast(I32), src[0].rearrange("p n t -> p (n t)").bitcast(I32))
             return tile
 
-        def load_scales(name, src, width, clear):
-            tile = sb.tile([P, width], U8, name=name, tag=name, align_bytes=64)
-            clear.memset(tile[:].bitcast(I32), 0)
-            nc.scalar.dma_start(tile[0:P:8, :].bitcast(I32), src[0].bitcast(I32))
-            return tile
-
-        def place_scale_rows(name, picked, width, queue):
-            placed = sb.tile([P, width], U8, name=name, align_bytes=64)
-            nc.gpsimd.memset(placed[:].bitcast(I32), 0)
+        def place_scale_rows(name, picked, queue):
+            placed = sb.tile([P, S], U8, name=name, align_bytes=64)
+            nc.vector.memset(placed[:].bitcast(I32), 0)
             for r in range(4):
                 queue.dma_start(placed[r:P:32, :].bitcast(I32), picked[8 * r:P:32, :].bitcast(I32))
             return placed
 
-        xs_table = load_scales("xs_table", x_scales, T, nc.gpsimd)
-        ds_table = load_scales("ds_table", d_scales, G, nc.vector)
+        ds_table = sb.tile([P, G], U8, name="ds_table", tag="ds_table", align_bytes=64)
+        nc.gpsimd.memset(ds_table[:].bitcast(I32), 0)
+        xs_table = sb.tile([P, T], U8, name="xs_table", align_bytes=64)
+        nc.vector.memset(xs_table[:].bitcast(I32), 0)
+        nc.scalar.dma_start(xs_table[0:P:8, :].bitcast(I32), x_scales[0].bitcast(I32))
+        offs_t = load_list("offs_t", offs)
+        ci_t = load_list("ci_t", ci)
+        for r in range(4):
+            queue = nc.sync if r < 2 else nc.scalar
+            queue.dma_start(ds_table[r:P:32, :].bitcast(I32), d_scales[0][r:16:4, :].bitcast(I32))
+        d_table = load_words("d_table", d_words, G)
         one = sb.tile([P, 1], F32, name="one")
         nc.vector.memset(one[:], 1.0)
         root_of_one = sb.tile([P, 1], F32, name="root_of_one")
         nc.scalar.activation(root_of_one[:], one[:], ACT.Sqrt)
-        offs_t = load_list("offs_t", offs)
-        ci_t = load_list("ci_t", ci)
-        d_table = load_words("d_table", d_words, G)
+        x_table = load_words("x_table", x_words, T)
         n1_t = load_list("n1_t", n1)
         n2_t = load_list("n2_t", n2)
         hz_t = load_list("hz_t", hz)
-        x_table = load_words("x_table", x_words, T)
         n3_t = load_list("n3_t", n3)
         n4_t = load_list("n4_t", n4)
         n5_t = load_list("n5_t", n5)
         gain = sb.tile([P, PACK], F32, name="gain")
-        nc.gpsimd.dma_start(gain[:], gn.rearrange("(p t) o -> p (t o)", t=PACK))
+        nc.sync.dma_start(gain[:], gn.rearrange("(p t) o -> p (t o)", t=PACK))
 
-        bytes1 = sb.tile([P, H + S], U8, name="bytes1", align_bytes=64)
-        nc.vector.tensor_copy(bytes1[:, H:], xs_table[:].indirect(offs_t[:]))
-        nc.vector.tensor_copy(bytes1[:, :H].rearrange("p (t m) -> p m t", t=PACK), ds_table[:].indirect(ci_t[:]))
-        scale1 = place_scale_rows("scale1", bytes1, H + S, nc.scalar)
+        x_bytes = sb.tile([P, S], U8, name="x_bytes", align_bytes=64)
+        nc.vector.tensor_copy(x_bytes[:], xs_table[:].indirect(offs_t[:]))
+        x_scale = place_scale_rows("x_scale", x_bytes, nc.scalar)
+        d_scale = sb.tile([P, H], U8, name="d_scale", align_bytes=64)
+        nc.vector.tensor_copy(d_scale[:].rearrange("p (t m) -> p m t", t=PACK), ds_table[:].indirect(ci_t[:]))
         d_codes = sb.tile([P, H], U32, name="d_codes", align_bytes=64)
         nc.vector.tensor_copy(d_codes[:].rearrange("p (t m) -> p m t", t=PACK), d_table[:].indirect(ci_t[:]))
         x_codes = sb.tile([P, S], U32, name="x_codes", align_bytes=64)
-        nc.vector.tensor_copy(x_codes[:], x_table[:].indirect(offs_t[:]))
+        for h in range(2):
+            nc.vector.tensor_copy(x_codes[:, HALF * h:HALF * (h + 1)], x_table[:].indirect(offs_t[:, 8 * h:8 * (h + 1)]))
 
         w2_raw = sb.tile([P, PACK, N], F32, name="w2_raw", tag="ds_table", align_bytes=64)
         nc.sync.dma_start(w2_raw[:], w2.rearrange("(p j) n -> p j n", j=PACK))
         w1_raw = sb.tile([P, PACK, N], F32, name="w1_raw", tag="d_table", align_bytes=64)
         nc.sync.dma_start(w1_raw[:], w1.rearrange("(p j) n -> p j n", j=PACK))
 
-        s_t = []
-        for t in range(PACK):
-            bank = psum.tile([P, S], F32, name="s_bank%d" % t, tag="bank%d" % t)
-            cols = slice(P * t, P * (t + 1))
+        def score(t, cols, tag):
+            bank = psum.tile([P, cols.stop - cols.start], F32, name="s_" + tag, tag=tag)
+            rows = slice(P * t, P * (t + 1))
             nc.tensor.matmul_mx(
-                out=bank[:], lhsT=d_codes[:, cols].bitcast(FP8X4), lhsT_scale=scale1[:, cols],
-                rhs=x_codes[:].bitcast(FP8X4), rhs_scale=scale1[:, H:], start=True, stop=True,
+                out=bank[:], lhsT=d_codes[:, rows].bitcast(FP8X4), lhsT_scale=d_scale[:, rows],
+                rhs=x_codes[:, cols].bitcast(FP8X4), rhs_scale=x_scale[:, cols], start=True, stop=True,
             )
-            s = sb.tile([P, S + SPARE], F32, name="s%d" % t)
-            nc.gpsimd.memset(s[:, S:], 0.0)
-            nc.vector.tensor_scalar(s[:, :S], bank[:], 0.0625, None, ALU.mult)
-            s_t.append(s)
+            return bank
+
+        s_t = [sb.tile([P, S + SPARE], F32, name="s%d" % t) for t in range(PACK)]
+        for s in s_t:
+            nc.vector.memset(s[:, S:], 0.0)
+        nc.scalar.activation(s_t[0][:, :HALF], score(0, slice(0, HALF), "first_bank")[:], ACT.Copy, scale=0.0625)
+        nc.vector.tensor_scalar(s_t[0][:, HALF:S], score(0, slice(HALF, S), "bank0")[:], 0.0625, None, ALU.mult)
+        for t in range(1, PACK):
+            nc.vector.tensor_scalar(s_t[t][:, :S], score(t, slice(0, S), "bank%d" % t)[:], 0.0625, None, ALU.mult)
 
         bytes2 = sb.tile([P, S], U8, name="bytes2", align_bytes=64)
         nc.vector.tensor_copy(bytes2[:], xs_table[:].indirect(hz_t[:]))
-        scale2 = place_scale_rows("scale2", bytes2, S, nc.sync)
+        scale2 = place_scale_rows("scale2", bytes2, nc.sync)
         hz_codes = sb.tile([P, S], U32, name="hz_codes", align_bytes=64)
         nc.vector.tensor_copy(hz_codes[:], x_table[:].indirect(hz_t[:]))
 
@@ -123,13 +129,18 @@ def tile_picked_xhznhsndminpolar_none_p_kernel(
         for t in range(PACK):
             cols = slice(S * t, S * (t + 1))
             ds = sb.tile([P, 2 * S], F32, name="ds%d" % t)
-            nc.scalar.activation(ds[:].indirect(n1_t[:]), s_t[t][:, :S], ACT.Copy)
             s2 = sb.tile([P, S], F32, name="s2_%d" % t)
-            nc.scalar.activation(s2[:], s_t[t][:].indirect(n2_t[:]), ACT.Copy)
+            if t == 0:
+                nc.scalar.activation(ds[:].indirect(n1_t[:, :8]), s_t[t][:, :HALF], ACT.Copy)
+                nc.scalar.activation(s2[:], s_t[t][:].indirect(n2_t[:]), ACT.Copy)
+                nc.scalar.activation(ds[:].indirect(n1_t[:, 8:]), s_t[t][:, HALF:S], ACT.Copy)
+            else:
+                nc.scalar.activation(ds[:].indirect(n1_t[:]), s_t[t][:, :S], ACT.Copy)
+                nc.scalar.activation(s2[:], s_t[t][:].indirect(n2_t[:]), ACT.Copy)
             nc.vector.tensor_tensor(st[:, cols], ds[:, :S], s2[:], ALU.min)
             nc.vector.tensor_scalar(stg[:, cols], st[:, cols], gain[:, t:t + 1], None, ALU.mult)
 
-        first_bank = psum.tile([P, PACK, HALF], F32, name="first_bank")
+        first_bank = psum.tile([P, PACK, HALF], F32, name="first_bank", tag="first_bank")
         acc = [[first_bank[:, m, :] for m in range(PACK)], []]
         for m in range(PACK):
             second_bank = psum.tile([P, HALF], F32, name="second_bank%d" % m, tag="bank%d" % m)

@@ -61,15 +61,9 @@ def tile_picked_xhznhsndminpolar_none_p_kernel(
         nc.vector.memset(one[:], 1.0)
         root_of_one = sb.tile([P, 1], F32, name="root_of_one")
         nc.scalar.activation(root_of_one[:], one[:], ACT.Sqrt)
-        x_table = load_words("x_table", x_words, T)
         n1_t = load_list("n1_t", n1)
         n2_t = load_list("n2_t", n2)
-        hz_t = load_list("hz_t", hz)
-        n3_t = load_list("n3_t", n3)
-        n4_t = load_list("n4_t", n4)
-        n5_t = load_list("n5_t", n5)
-        gain = sb.tile([P, PACK], F32, name="gain")
-        nc.sync.dma_start(gain[:], gn.rearrange("(p t) o -> p (t o)", t=PACK))
+        x_table = load_words("x_table", x_words, T)
 
         x_bytes = sb.tile([P, S], U8, name="x_bytes", align_bytes=64)
         nc.vector.tensor_copy(x_bytes[:], xs_table[:].indirect(offs_t[:]))
@@ -84,8 +78,14 @@ def tile_picked_xhznhsndminpolar_none_p_kernel(
 
         w2_raw = sb.tile([P, PACK, N], F32, name="w2_raw", tag="ds_table", align_bytes=64)
         nc.sync.dma_start(w2_raw[:], w2.rearrange("(p j) n -> p j n", j=PACK))
+        hz_t = load_list("hz_t", hz)
         w1_raw = sb.tile([P, PACK, N], F32, name="w1_raw", tag="d_table", align_bytes=64)
         nc.sync.dma_start(w1_raw[:], w1.rearrange("(p j) n -> p j n", j=PACK))
+        gain = sb.tile([P, PACK], F32, name="gain")
+        nc.sync.dma_start(gain[:], gn.rearrange("(p t) o -> p (t o)", t=PACK))
+        n3_t = load_list("n3_t", n3)
+        n4_t = load_list("n4_t", n4)
+        n5_t = load_list("n5_t", n5)
 
         def score(t, cols, tag):
             bank = psum.tile([P, cols.stop - cols.start], F32, name="s_" + tag, tag=tag)
@@ -124,7 +124,7 @@ def tile_picked_xhznhsndminpolar_none_p_kernel(
         w2_codes, w2_scales = quantise_weight("w2", w2_raw)
         w1_codes, w1_scales = quantise_weight("w1", w1_raw)
 
-        st = sb.tile([P, PACK * S], F32, name="st", tag="stage", align_bytes=64)
+        st = sb.tile([P, PACK * S], F32, name="st", tag="d_table", align_bytes=64)
         stg = sb.tile([P, PACK * S], F32, name="stg")
         for t in range(PACK):
             cols = slice(S * t, S * (t + 1))
@@ -155,21 +155,21 @@ def tile_picked_xhznhsndminpolar_none_p_kernel(
                     start=(h == 1 or m == 0), stop=False,
                 )
 
-        h2 = sb.tile([P, PACK * S], F32, name="h2")
-        h2_view = h2[:].rearrange("p (m c) -> p m c", m=PACK)
+        h2 = [sb.tile([P, S], F32, name="h2_%d" % m) for m in range(PACK)]
         for h in range(2):
             st3 = sb.tile([P, PACK * HALF], F32, name="st3_%d" % h)
+            z_rows = sb.tile([P, PACK * HALF], BF16, name="z_rows%d" % h)
             for t in range(PACK):
+                piece = slice(HALF * t, HALF * (t + 1))
                 nc.scalar.activation(
-                    st3[:, HALF * t:HALF * (t + 1)],
-                    stg[:, S * t:S * (t + 1)].indirect(n3_t[:, 8 * h:8 * (h + 1)]), ACT.Copy,
+                    st3[:, piece], stg[:, S * t:S * (t + 1)].indirect(n3_t[:, 8 * h:8 * (h + 1)]), ACT.Copy,
                 )
+                start = S * t + HALF * h
+                nc.vector.tensor_tensor(z_rows[:, piece], stg[:, start:start + HALF], st3[:, piece], ALU.subtract)
             z = sb.tile([P, HALF * PACK], BF16, name="z%d" % h, align_bytes=64)
-            nc.vector.tensor_tensor(
+            nc.vector.tensor_copy(
                 z[:].rearrange("p (c i t) -> p c t i", i=4, t=PACK),
-                stg[:].rearrange("p (t h c i) -> p h c t i", t=PACK, h=2, i=4)[:, h],
-                st3[:].rearrange("p (t c i) -> p c t i", t=PACK, i=4),
-                ALU.subtract,
+                z_rows[:].rearrange("p (t c i) -> p c t i", t=PACK, i=4),
             )
             z_codes = sb.tile([P, HALF], U32, name="z_codes%d" % h, align_bytes=64)
             z_scales = sb.tile([P, HALF], U8, name="z_scales%d" % h, align_bytes=64)
@@ -181,10 +181,11 @@ def tile_picked_xhznhsndminpolar_none_p_kernel(
                     rhs=z_codes[:].bitcast(FP8X4), rhs_scale=z_scales[:],
                     start=False, stop=(h == 1 or m == PACK - 1),
                 )
-        nc.scalar.copy(h2_view[:, :, :HALF], first_bank[:])
-        nc.scalar.copy(h2_view[:, 0, HALF:], acc[1][0])
+        for m in range(PACK):
+            nc.scalar.copy(h2[m][:, :HALF], acc[0][m])
+        nc.scalar.copy(h2[0][:, HALF:], acc[1][0])
         for m in range(1, PACK):
-            nc.vector.tensor_copy(h2_view[:, m, HALF:], acc[1][m])
+            nc.vector.tensor_copy(h2[m][:, HALF:], acc[1][m])
 
         pairs = sb.tile([P, PACK, 2, W], F32, name="pairs")
         squares = sb.tile([P, PACK, 2, W], F32, name="squares")
@@ -192,7 +193,7 @@ def tile_picked_xhznhsndminpolar_none_p_kernel(
         rb = sb.tile([P, PACK, W], F32, name="rb")
         ra = sb.tile([P, PACK * W], F32, name="ra")
         for m in range(PACK):
-            window = h2[:, S * m:S * (m + 1)]
+            window = h2[m][:]
             nc.scalar.activation(pairs[:, m, 0, :], window.indirect(n4_t[:]), ACT.Copy)
             nc.scalar.activation(pairs[:, m, 1, :], window.indirect(n5_t[:]), ACT.Copy)
             nc.vector.scalar_tensor_tensor(rb[:, m, :], pairs[:, m, 0, :], -0.5, pairs[:, m, 1, :], ALU.mult, ALU.add)

from contextlib import ExitStack

import concourse.mybir as mybir

F32 = mybir.dt.float32
BF16 = mybir.dt.bfloat16
I32 = mybir.dt.int32
U32 = mybir.dt.uint32
U16 = mybir.dt.uint16
U8 = mybir.dt.uint8
FP8X4 = mybir.dt.float8_e4m3fn_x4
ALU = mybir.AluOpType
ACT = mybir.ActivationFunctionType

P = 128
PACK = 4
K, T, S, N, G, H, W = 512, 1024, 256, 512, 2048, 512, 128
HALF = S // 2
SPARE = 16
FLOPS = 2 * S * (K * H + H * N + K * N)


def tile_picked_xhznhsndminpolar_none_p_kernel(
    tc, x_words, x_scales, d_words, d_scales, gn, w1, w2, offs, ci, n1, n2, n3, hz, n4, n5, out
):
    nc = tc.nc
    with ExitStack() as ctx:
        lists = ctx.enter_context(tc.tile_pool(name="lists", bufs=1))
        sb = ctx.enter_context(tc.tile_pool(name="sb", bufs=1))
        psum = ctx.enter_context(tc.psum_pool(name="psum", bufs=1))

        def load_list(name, src):
            tile = lists.tile(list(src.shape), U16, name=name)
            nc.sync.dma_start(tile[:], src)
            return tile

        def load_words(name, src, width):
            tile = sb.tile([P, width], U32, name=name, tag=name, align_bytes=64)
            nc.sync.dma_start(tile[:].bitcast(I32), src[0].rearrange("p n t -> p (n t)").bitcast(I32))
            return tile

        def place_scale_rows(name, picked, queue):
            placed = sb.tile([P, S], U8, name=name, align_bytes=64)
            nc.vector.memset(placed[:].bitcast(I32), 0)
            for r in range(4):
                queue.dma_start(placed[r:P:32, :].bitcast(I32), picked[8 * r:P:32, :].bitcast(I32))
            return placed

        ds_table = sb.tile([P, G], U8, name="ds_table", tag="ds_table", align_bytes=64)
        nc.gpsimd.memset(ds_table[:].bitcast(I32), 0)
        xs_table = sb.tile([P, T], U8, name="xs_table", align_bytes=64)
        nc.vector.memset(xs_table[:].bitcast(I32), 0)
        nc.scalar.dma_start(xs_table[0:P:8, :].bitcast(I32), x_scales[0].bitcast(I32))
        offs_t = load_list("offs_t", offs)
        ci_t = load_list("ci_t", ci)
        for r in range(4):
            queue = nc.sync if r < 2 else nc.scalar
            queue.dma_start(ds_table[r:P:32, :].bitcast(I32), d_scales[0][r:16:4, :].bitcast(I32))
        d_table = load_words("d_table", d_words, G)
        one = sb.tile([P, 1], F32, name="one")
        nc.vector.memset(one[:], 1.0)
        root_of_one = sb.tile([P, 1], F32, name="root_of_one")
        nc.scalar.activation(root_of_one[:], one[:], ACT.Sqrt)
        n1_t = load_list("n1_t", n1)
        n2_t = load_list("n2_t", n2)
        x_table = load_words("x_table", x_words, T)

        x_bytes = sb.tile([P, S], U8, name="x_bytes", align_bytes=64)
        nc.vector.tensor_copy(x_bytes[:], xs_table[:].indirect(offs_t[:]))
        x_scale = place_scale_rows("x_scale", x_bytes, nc.scalar)
        d_scale = sb.tile([P, H], U8, name="d_scale", align_bytes=64)
        nc.vector.tensor_copy(d_scale[:].rearrange("p (t m) -> p m t", t=PACK), ds_table[:].indirect(ci_t[:]))
        d_codes = sb.tile([P, H], U32, name="d_codes", align_bytes=64)
        nc.vector.tensor_copy(d_codes[:].rearrange("p (t m) -> p m t", t=PACK), d_table[:].indirect(ci_t[:]))
        x_codes = sb.tile([P, S], U32, name="x_codes", align_bytes=64)
        for h in range(2):
            nc.vector.tensor_copy(x_codes[:, HALF * h:HALF * (h + 1)], x_table[:].indirect(offs_t[:, 8 * h:8 * (h + 1)]))

        w2_raw = sb.tile([P, PACK, N], F32, name="w2_raw", tag="ds_table", align_bytes=64)
        nc.sync.dma_start(w2_raw[:], w2.rearrange("(p j) n -> p j n", j=PACK))
        hz_t = load_list("hz_t", hz)
        w1_raw = sb.tile([P, PACK, N], F32, name="w1_raw", tag="d_table", align_bytes=64)
        nc.sync.dma_start(w1_raw[:], w1.rearrange("(p j) n -> p j n", j=PACK))
        gain = sb.tile([P, PACK], F32, name="gain")
        nc.sync.dma_start(gain[:], gn.rearrange("(p t) o -> p (t o)", t=PACK))
        n3_t = load_list("n3_t", n3)
        n4_t = load_list("n4_t", n4)
        n5_t = load_list("n5_t", n5)

        def score(t, cols, tag):
            bank = psum.tile([P, cols.stop - cols.start], F32, name="s_" + tag, tag=tag)
            rows = slice(P * t, P * (t + 1))
            nc.tensor.matmul_mx(
                out=bank[:], lhsT=d_codes[:, rows].bitcast(FP8X4), lhsT_scale=d_scale[:, rows],
                rhs=x_codes[:, cols].bitcast(FP8X4), rhs_scale=x_scale[:, cols], start=True, stop=True,
            )
            return bank

        s_t = [sb.tile([P, S + SPARE], F32, name="s%d" % t) for t in range(PACK)]
        for s in s_t:
            nc.vector.memset(s[:, S:], 0.0)
        nc.scalar.activation(s_t[0][:, :HALF], score(0, slice(0, HALF), "first_bank")[:], ACT.Copy, scale=0.0625)
        nc.vector.tensor_scalar(s_t[0][:, HALF:S], score(0, slice(HALF, S), "bank0")[:], 0.0625, None, ALU.mult)
        for t in range(1, PACK):
            nc.vector.tensor_scalar(s_t[t][:, :S], score(t, slice(0, S), "bank%d" % t)[:], 0.0625, None, ALU.mult)

        bytes2 = sb.tile([P, S], U8, name="bytes2", align_bytes=64)
        nc.vector.tensor_copy(bytes2[:], xs_table[:].indirect(hz_t[:]))
        scale2 = place_scale_rows("scale2", bytes2, nc.sync)
        hz_codes = sb.tile([P, S], U32, name="hz_codes", align_bytes=64)
        nc.vector.tensor_copy(hz_codes[:], x_table[:].indirect(hz_t[:]))

        def quantise_weight(name, raw):
            grouped = sb.tile([P, N * PACK], BF16, name=name + "_grouped", tag="stage", align_bytes=64)
            nc.vector.tensor_copy(
                grouped[:].rearrange("p (c i t) -> p c t i", i=4, t=PACK),
                raw[:].rearrange("p t (c i) -> p c t i", i=4),
            )
            codes = sb.tile([P, N], U32, name=name + "_codes", align_bytes=64)
            scales = sb.tile([P, N], U8, name=name + "_scales", align_bytes=64)
            nc.vector.quantize_mx(out=codes[:].bitcast(FP8X4), scales=scales[:], in_=grouped[:])
            return codes, scales

        w2_codes, w2_scales = quantise_weight("w2", w2_raw)
        w1_codes, w1_scales = quantise_weight("w1", w1_raw)

        st = sb.tile([P, PACK * S], F32, name="st", tag="d_table", align_bytes=64)
        stg = sb.tile([P, PACK * S], F32, name="stg")
        for t in range(PACK):
            cols = slice(S * t, S * (t + 1))
            ds = sb.tile([P, 2 * S], F32, name="ds%d" % t)
            s2 = sb.tile([P, S], F32, name="s2_%d" % t)
            if t == 0:
                nc.scalar.activation(ds[:].indirect(n1_t[:, :8]), s_t[t][:, :HALF], ACT.Copy)
                nc.scalar.activation(s2[:], s_t[t][:].indirect(n2_t[:]), ACT.Copy)
                nc.scalar.activation(ds[:].indirect(n1_t[:, 8:]), s_t[t][:, HALF:S], ACT.Copy)
            else:
                nc.scalar.activation(ds[:].indirect(n1_t[:]), s_t[t][:, :S], ACT.Copy)
                nc.scalar.activation(s2[:], s_t[t][:].indirect(n2_t[:]), ACT.Copy)
            nc.vector.tensor_tensor(st[:, cols], ds[:, :S], s2[:], ALU.min)
            nc.vector.tensor_scalar(stg[:, cols], st[:, cols], gain[:, t:t + 1], None, ALU.mult)

        first_bank = psum.tile([P, PACK, HALF], F32, name="first_bank", tag="first_bank")
        acc = [[first_bank[:, m, :] for m in range(PACK)], []]
        for m in range(PACK):
            second_bank = psum.tile([P, HALF], F32, name="second_bank%d" % m, tag="bank%d" % m)
            acc[1].append(second_bank[:])
        for h in range(2):
            for m in range(PACK):
                rows = slice(P * m, P * (m + 1))
                cols = slice(HALF * h, HALF * (h + 1))
                nc.tensor.matmul_mx(
                    out=acc[h][m], lhsT=w2_codes[:, rows].bitcast(FP8X4), lhsT_scale=w2_scales[:, rows],
                    rhs=hz_codes[:, cols].bitcast(FP8X4), rhs_scale=scale2[:, cols],
                    start=(h == 1 or m == 0), stop=False,
                )

        h2 = [sb.tile([P, S], F32, name="h2_%d" % m) for m in range(PACK)]
        for h in range(2):
            st3 = sb.tile([P, PACK * HALF], F32, name="st3_%d" % h)
            z_rows = sb.tile([P, PACK * HALF], BF16, name="z_rows%d" % h)
            for t in range(PACK):
                piece = slice(HALF * t, HALF * (t + 1))
                nc.scalar.activation(
                    st3[:, piece], stg[:, S * t:S * (t + 1)].indirect(n3_t[:, 8 * h:8 * (h + 1)]), ACT.Copy,
                )
                start = S * t + HALF * h
                nc.vector.tensor_tensor(z_rows[:, piece], stg[:, start:start + HALF], st3[:, piece], ALU.subtract)
            z = sb.tile([P, HALF * PACK], BF16, name="z%d" % h, align_bytes=64)
            nc.vector.tensor_copy(
                z[:].rearrange("p (c i t) -> p c t i", i=4, t=PACK),
                z_rows[:].rearrange("p (t c i) -> p c t i", t=PACK, i=4),
            )
            z_codes = sb.tile([P, HALF], U32, name="z_codes%d" % h, align_bytes=64)
            z_scales = sb.tile([P, HALF], U8, name="z_scales%d" % h, align_bytes=64)
            nc.vector.quantize_mx(out=z_codes[:].bitcast(FP8X4), scales=z_scales[:], in_=z[:])
            for m in range(PACK):
                rows = slice(P * m, P * (m + 1))
                nc.tensor.matmul_mx(
                    out=acc[h][m], lhsT=w1_codes[:, rows].bitcast(FP8X4), lhsT_scale=w1_scales[:, rows],
                    rhs=z_codes[:].bitcast(FP8X4), rhs_scale=z_scales[:],
                    start=False, stop=(h == 1 or m == PACK - 1),
                )
        for m in range(PACK):
            nc.scalar.copy(h2[m][:, :HALF], acc[0][m])
        nc.scalar.copy(h2[0][:, HALF:], acc[1][0])
        for m in range(1, PACK):
            nc.vector.tensor_copy(h2[m][:, HALF:], acc[1][m])

        pairs = sb.tile([P, PACK, 2, W], F32, name="pairs")
        squares = sb.tile([P, PACK, 2, W], F32, name="squares")
        radicand = sb.tile([P, PACK * W], F32, name="radicand")
        rb = sb.tile([P, PACK, W], F32, name="rb")
        ra = sb.tile([P, PACK * W], F32, name="ra")
        for m in range(PACK):
            window = h2[m][:]
            nc.scalar.activation(pairs[:, m, 0, :], window.indirect(n4_t[:]), ACT.Copy)
            nc.scalar.activation(pairs[:, m, 1, :], window.indirect(n5_t[:]), ACT.Copy)
            nc.vector.scalar_tensor_tensor(rb[:, m, :], pairs[:, m, 0, :], -0.5, pairs[:, m, 1, :], ALU.mult, ALU.add)
            nc.vector.tensor_tensor(squares[:, m], pairs[:, m], pairs[:, m], ALU.mult)
            nc.vector.scalar_tensor_tensor(
                radicand[:, W * m:W * (m + 1)], squares[:, m, 0, :], 0.25, squares[:, m, 1, :], ALU.add, ALU.add
            )
        results = [sb.tile([P, S], F32, name="result%d" % m) for m in range(PACK)]
        for m in range(2):
            nc.scalar.activation(results[m][:].indirect(n5_t[:]), rb[:, m, :], ACT.Copy)
        nc.scalar.activation(ra[:], radicand[:], ACT.Sqrt)
        for m in range(PACK):
            nc.scalar.activation(results[m][:].indirect(n4_t[:]), ra[:, W * m:W * (m + 1)], ACT.Copy)
            nc.sync.dma_start(out[P * m:P * (m + 1), :], results[m][:])
            if m + 2 < PACK:
                nc.scalar.activation(results[m + 2][:].indirect(n5_t[:]), rb[:, m + 2, :], ACT.Copy)
